import numpy as np, ml_dtypes
CORES = [29,45,93,109,157,173,221,237,285,301,349,365,413,429,477,493]
N = 16
import mx_ref
NC, G, KO, SH = 128, 2, 1, 3
C = np.float32(0.019)
BF = ml_dtypes.bfloat16
def cut(t, i, w=512):
    return t[:, w * i:w * i + w]
def tile(rs):
    return np.stack(rs, axis=2).reshape(128, -1).astype(BF)
def layer(w, X):
    out = []
    for i in range(G):
        for t in range(len(X)):
            p = mx_ref.matmul(mx_ref.quantize(cut(w, len(X) * i + t)), X[t])
            z = p if t == 0 else z + p
        out.append(z)
    return out
def act(Z):
    return [np.maximum(s * z, 0) * C for z in Z for s in (1, -1)]
def inputs(rng, e, E):
    def f(*shape):
        v = (rng.standard_normal(shape, dtype=np.float32) * np.exp2(rng.integers(-2, 3, shape[:-1] + (1,)))).astype(BF)
        return mx_ref.spread((v.astype(np.float32) * np.exp2(rng.integers(-E, E + 1, shape[:-2] + (1, 1))).astype(np.float32)).astype(BF), rng, e)
    def packed(k):
        c = np.zeros((N, 128, k * 512), np.uint8); s = np.zeros((N, 128, k * 128), np.uint8)
        for r in range(N):
            for i in range(k):
                a, b = mx_ref.quantize(f(128, 512)); c[r][:, 512 * i:512 * i + 512] = a; s[r][:, 128 * i:128 * i + 128] = mx_ref.plane(b, rng)
        return c, s
    d = {}
    d["kc"], d["ks"] = packed(KO)
    d["x"] = f(N, 128, 4 * NC)
    d["wk"] = f(N, 128, G * 512)
    d["q"] = f(N, 128, 512)
    return d
def setup_inputs(rng):
    return inputs(rng, 0, 0)
def setup_inputs_blocks(rng):
    return inputs(rng, 4, 0)
def setup_inputs_wide(rng):
    return inputs(rng, 0, 8)
def reference(kc, ks, x, wk, q):
    new = [mx_ref.quantize(tile(act(layer(wk[r], [mx_ref.quantize(x[r])])))) for r in range(N)]
    y = np.zeros((N, 128, 128 * KO + NC), np.float32)
    for o in range(N):
        old = (np.ascontiguousarray(kc[o]), mx_ref.live(ks[o]))
        qq = mx_ref.quantize(q[o])
        y[o] = np.concatenate([mx_ref.matmul(qq, old), mx_ref.matmul(qq, new[(o - SH) % N])], axis=1)
    return {"y": y}

from concourse.mybir import dt, AluOpType, ActivationFunctionType

NCOL = 128
W = 4 * NCOL
C = 0.019
SH = 3
BANK = 512

SCRATCH = {
    "xt": ("sbuf", [128, W], "bfloat16"),
    "w0": ("sbuf", [128, W], "bfloat16"),
    "w1": ("sbuf", [128, W], "bfloat16"),
    "qt": ("sbuf", [128, W], "bfloat16"),
    "kt": ("sbuf", [128, W], "bfloat16"),
    "xc": ("sbuf", [128, NCOL], "float8_e4m3fn_x4"), "xs": ("sbuf", [128, NCOL], "uint8"),
    "w0c": ("sbuf", [128, NCOL], "float8_e4m3fn_x4"), "w0s": ("sbuf", [128, NCOL], "uint8"),
    "w1c": ("sbuf", [128, NCOL], "float8_e4m3fn_x4"), "w1s": ("sbuf", [128, NCOL], "uint8"),
    "qc": ("sbuf", [128, NCOL], "float8_e4m3fn_x4"), "qs": ("sbuf", [128, NCOL], "uint8"),
    "okc": ("sbuf", [128, NCOL], "float8_e4m3fn_x4"), "oks": ("sbuf", [128, NCOL], "uint8"),
    "mkc": ("sbuf", [128, NCOL], "float8_e4m3fn_x4"), "mks": ("sbuf", [128, NCOL], "uint8"),
    "nkc": ("sbuf", [128, NCOL], "float8_e4m3fn_x4"), "nks": ("sbuf", [128, NCOL], "uint8"),
    "z": ("psum", [128, 4 * BANK], "float32"),
    "yo": ("sbuf", [128, NCOL], "float32"),
    "yn": ("sbuf", [128, NCOL], "float32"),
}
SEMAPHORES = ["lx", "lw0", "lw1", "lq", "lk", "qx", "qw0", "qw1", "qq", "z0", "z1", "zo", "zn", "t0", "t1", "made", "sent",
              "arrived", "co", "cn", "stored"]


def rank_program(g, core, T, topo):
    rank = T.rank_of(core)
    if rank is None:
        return
    n = len(T.cores)
    owner = T.cores[(rank + SH) % n]
    maker = T.cores[(rank - SH) % n]
    S = T.sem
    z0, z1 = T.z[:, 0:NCOL], T.z[:, BANK:BANK + NCOL]
    zo, zn = T.z[:, 2 * BANK:2 * BANK + NCOL], T.z[:, 3 * BANK:3 * BANK + NCOL]
    send_mask, recv_mask = topo.mask(core, owner), topo.mask(maker, core)

    g.sync.dma_start(T.xt[:], T.x[:]).then_inc(S.lx, 16)
    g.scalar.dma_start(T.w0[:], T.wk[:, 0:W]).then_inc(S.lw0, 16)
    g.sync.dma_start(T.w1[:], T.wk[:, W:2 * W]).then_inc(S.lw1, 16)
    g.scalar.dma_start(T.qt[:], T.q[:]).then_inc(S.lq, 16)
    g.sync.dma_start(T.okc[:].bitcast(dt.uint8), T.kc[:]).then_inc(S.lk, 16)
    g.sync.dma_start(T.oks[:], T.ks[:]).then_inc(S.lk, 16)

    v = g.vector
    v.wait_ge(S.lx, 16)
    v.quantize_mx(T.xc[:], T.xs[:], T.xt[:]).then_inc(S.qx, 1)
    v.wait_ge(S.lw0, 16)
    v.quantize_mx(T.w0c[:], T.w0s[:], T.w0[:]).then_inc(S.qw0, 1)
    v.wait_ge(S.lw1, 16)
    v.quantize_mx(T.w1c[:], T.w1s[:], T.w1[:]).then_inc(S.qw1, 1)
    v.wait_ge(S.z1, 1)
    v.tensor_scalar(T.kt[:, 2:W:4], z1, 0.0, C, AluOpType.max, AluOpType.mult).then_inc(S.t1, 1)
    v.tensor_scalar(T.kt[:, 3:W:4], z1, -C, 0.0, AluOpType.mult, AluOpType.max).then_inc(S.t1, 1)
    v.wait_ge(S.t0, 2)
    v.wait_ge(S.t1, 2)
    v.quantize_mx(T.mkc[:], T.mks[:], T.kt[:]).then_inc(S.made, 1)
    v.wait_ge(S.lq, 16)
    v.quantize_mx(T.qc[:], T.qs[:], T.qt[:]).then_inc(S.qq, 1)
    v.wait_ge(S.zn, 1)
    v.tensor_copy(T.yn[:], zn).then_inc(S.cn, 1)

    t = g.tensor
    t.wait_ge(S.qx, 1)
    t.wait_ge(S.qw0, 1)
    t.matmul_mx(z0, T.w0c[:], T.w0s[:], T.xc[:], T.xs[:], True, True).then_inc(S.z0, 1)
    t.wait_ge(S.qw1, 1)
    t.matmul_mx(z1, T.w1c[:], T.w1s[:], T.xc[:], T.xs[:], True, True).then_inc(S.z1, 1)
    t.wait_ge(S.qq, 1)
    t.wait_ge(S.lk, 32)
    t.matmul_mx(zo, T.qc[:], T.qs[:], T.okc[:], T.oks[:], True, True).then_inc(S.zo, 1)
    t.wait_ge(S.arrived, 2 * bin(recv_mask).count("1"))
    t.matmul_mx(zn, T.qc[:], T.qs[:], T.nkc[:], T.nks[:], True, True).then_inc(S.zn, 1)

    a = g.scalar
    a.wait_ge(S.z0, 1)
    a.activation(T.kt[:, 0:W:4], z0, ActivationFunctionType.Relu, scale=C).then_inc(S.t0, 1)
    a.activation(T.kt[:, 1:W:4], z0, ActivationFunctionType.Relu, scale=-C).then_inc(S.t0, 1)
    a.wait_ge(S.zo, 1)
    a.activation(T.yo[:], zo, ActivationFunctionType.Copy).then_inc(S.co, 1)

    rid, pid = topo.addr(owner, core)
    g.wait_ge(S.made, 1)
    g.remote_dma(out_ap=T.nkc[:].bitcast(dt.uint8), in_ap=T.mkc[:].bitcast(dt.uint8), remote_sem=S.arrived, local_sem=S.sent,
                 pid=pid, routing_id=rid, dma_engine_mask=send_mask)
    g.remote_dma(out_ap=T.nks[:], in_ap=T.mks[:], remote_sem=S.arrived, local_sem=S.sent,
                 pid=pid, routing_id=rid, dma_engine_mask=send_mask)
    g.wait_ge(S.sent, 2 * bin(send_mask).count("1"))

    s = g.sync
    s.wait_ge(S.co, 1)
    s.dma_start(T.y[:, 0:NCOL], T.yo[:]).then_inc(S.stored, 16)
    s.wait_ge(S.cn, 1)
    s.dma_start(T.y[:, NCOL:2 * NCOL], T.yn[:]).then_inc(S.stored, 16)
    s.wait_ge(S.stored, 32)
